import numpy as np
import ml_dtypes


def mxq(x, axis, fmt="e4m3"):
    dtype, down = {"e4m3": (ml_dtypes.float8_e4m3fn, 7), "e5m2": (ml_dtypes.float8_e5m2, 14)}[fmt]
    v = np.moveaxis(np.asarray(x, np.float32).astype(ml_dtypes.bfloat16).astype(np.float64), axis, -1)
    blocks = v.reshape(v.shape[:-1] + (-1, 32))
    amax = np.abs(blocks).max(-1, keepdims=True)
    byte = np.maximum(np.where(amax > 0, np.frexp(amax)[1] - 1 + 127, 0) - down, 1)
    scale = np.exp2(byte - 127.0)
    codes = (blocks / scale).astype(np.float32).astype(dtype).astype(np.float64)
    return np.moveaxis((codes * scale).reshape(v.shape), -1, axis)


WIDE = False


def mx_kscale(k):
    if not WIDE:
        return np.ones(k)
    levels = np.array([10, -10, 5, -5, 0])
    if k % 512:
        return np.exp2(np.random.permutation(np.resize(levels, k // 32))).repeat(32)
    a = np.empty((k // 512, 16))
    for p in range(k // 512):
        a[p, :8] = np.random.permutation(np.resize(levels, 8))
        for g in range(8):
            far = levels[np.abs(levels - a[p, g]) >= 10]
            a[p, g + 8] = far[np.random.randint(len(far))]
    return np.exp2(a.ravel()).repeat(32)


def f64(x):
    return np.asarray(x).astype(np.float64)


def striped(idx):
    return np.tile(np.asarray(idx).reshape(-1, 16).T, (8, 1)).astype(np.uint16)


def unstriped(offs):
    return offs[:16].T.reshape(-1).astype(np.int64)


E2M1 = np.array([0.0, 0.5, 1.0, 1.5, 2.0, 3.0, 4.0, 6.0, -0.0, -0.5, -1.0, -1.5, -2.0, -3.0, -4.0, -6.0])


def pack_weight(w, fmt):
    k, n = w.shape
    w = f64(np.asarray(w, np.float32).astype(ml_dtypes.bfloat16)).reshape(k // 32, 32, n)
    amax = np.abs(w).max(1)
    if fmt == "e4m3":
        byte = np.frexp(amax)[1] - 1 + 127 - 7
    else:
        mant, ex = np.frexp(amax / 6.0)
        byte = np.where(mant > 0.5, ex, ex - 1) + 127
    byte = np.clip(np.where(amax > 0, byte, 1), 1, 254)
    scaled = (w * np.exp2(127.0 - byte)[:, None, :]).reshape(k, n).astype(np.float32)
    by_word = np.ascontiguousarray(scaled.reshape(k // 512, 128, 4, n).transpose(0, 1, 3, 2))
    if fmt == "e4m3":
        words = by_word.astype(ml_dtypes.float8_e4m3fn).view(np.uint8)
    else:
        c = by_word.astype(ml_dtypes.float4_e2m1fn).view(np.uint8) & 0xF
        words = (c[..., 0::2] | (c[..., 1::2] << 4)).reshape(k // 512, 128, 2 * n)
    return np.ascontiguousarray(words), np.ascontiguousarray(byte.astype(np.uint8).reshape(k // 512, 16, n))


def unpack_weight(words, scales, fmt):
    g, _, n = scales.shape
    words = np.ascontiguousarray(words).reshape(g, 128, n, -1)
    if fmt == "e4m3":
        vals = words.view(ml_dtypes.float8_e4m3fn).astype(np.float64)
    else:
        nib = np.empty((g, 128, n, 4), np.uint8)
        nib[..., 0::2] = words & 0xF
        nib[..., 1::2] = words >> 4
        vals = E2M1[nib]
    vals = vals * np.repeat(np.exp2(scales.astype(np.float64) - 127.0), 8, axis=1)[..., None]
    return vals.transpose(0, 1, 3, 2).reshape(g * 512, n)


def bf(x):
    return np.asarray(x, np.float32).astype(ml_dtypes.bfloat16)


def planes(Y):
    r, m = Y.shape
    b = f64(bf(Y)).reshape(r // 32, 32, m)
    amax = np.abs(b).max(1)
    byte = np.clip(np.where(amax > 0, np.frexp(amax)[1] - 1 + 127 - 7, 1), 1, 254)
    codes = (b * np.exp2(127.0 - byte)[:, None, :]).reshape(r, m).astype(np.float32).astype(ml_dtypes.float8_e4m3fn).view(np.uint8)
    words = codes.reshape(r // 512, 128, 4, m).transpose(0, 1, 3, 2)
    return np.ascontiguousarray(words), np.ascontiguousarray(byte.astype(np.uint8).reshape(r // 512, 16, m))


D, T, I, J, U, Z, M, N = 512, 2048, 512, 512, 1024, 1024, 512, 64


def setup_inputs():
    n = np.random.standard_normal
    idx = np.random.permutation(T)[:I]
    idx2 = np.random.permutation(U)[:J]
    idx3 = np.random.permutation(Z)[:J]
    idx4 = np.random.permutation(M)[:N]
    fd = mx_kscale(D)
    keysp = pack_weight(n((D, T)) / fd[:, None], "e2m1")
    return {
        "keys_words": keysp[0],
        "keys_scales": keysp[1],
        "notes": (n((D, U)) * 1.0 / np.sqrt(D) * fd[:, None]).astype(np.float32),
        "users2": (n((D, Z)) * 1.0 / np.sqrt(D) * fd[:, None]).astype(np.float32),
        "old": (1.0 * n((I, M))).astype(np.float32),
        "offs": striped(idx),
        "offs2": striped(idx2),
        "offs3": striped(idx3),
        "offs4": striped(idx4),
    }


def reference(keys_words, keys_scales, notes, users2, old, offs, offs2, offs3, offs4):
    idx = unstriped(offs)
    idx2 = unstriped(offs2)
    idx3 = unstriped(offs3)
    idx4 = unstriped(offs4)
    keysu = unpack_weight(keys_words, keys_scales, "e2m1")
    keysidxg = keysu[:, idx]
    notesq = mxq(f64(notes), 0, "e4m3")
    g1 = keysidxg.T @ notesq
    users2idx3q = mxq(f64(users2)[:, idx3], 0, "e4m3")
    g2 = keysidxg.T @ users2idx3q
    g0 = np.maximum(g1[:, idx2], g2)
    rb0 = g0.reshape(I, N, J // N).max(axis=2)
    gf = np.zeros((I, M))
    gf[:, idx4] = rb0
    y = f64(old) + gf
    words, scales = planes(y)
    return y, words, scales

@@ -1,0 +1,191 @@
+from contextlib import ExitStack
+
+import concourse.mybir as mybir
+
+D, T, I, J, U, Z, M, N = 512, 2048, 512, 512, 1024, 1024, 512, 64
+FLOPS = 2 * D * I * (U + J)
+
+F32 = mybir.dt.float32
+BF16 = mybir.dt.bfloat16
+I32 = mybir.dt.int32
+U32 = mybir.dt.uint32
+U16 = mybir.dt.uint16
+U8 = mybir.dt.uint8
+FP8X4 = mybir.dt.float8_e4m3fn_x4
+FP4X4 = mybir.dt.float4_e2m1fn_x4
+COPY = mybir.ActivationFunctionType.Copy
+MAX = mybir.AluOpType.max
+ADD = mybir.AluOpType.add
+AXIS_X = mybir.AxisListType.X
+
+P = 128
+PACK = 4
+BANK = 512
+RUN = J // N
+LINE = 4
+CHUNK = 256
+USERS_ON_SCALAR = 192
+RESULT_ON_SCALAR = 192
+
+
+def interleave(copy, words, planes, first, last):
+    copy(
+        out=words[:, first:last, :].rearrange("p (c i) t -> p c t i", i=LINE),
+        in_=planes[:, :, first:last].rearrange("p t (c i) -> p c t i", i=LINE),
+    )
+
+
+def quantize(nc, codes, scales, words):
+    nc.vector.quantize_mx(
+        out=codes[:].bitcast(FP8X4),
+        scales=scales[:],
+        in_=words[:].rearrange("p c t -> p (c t)"),
+    )
+
+
+def tile_attend_tab_wideandown_runsput_pl_kernel(
+    tc, keys_words, keys_scales, notes, users2, old, offs, offs2, offs3, offs4, out_0, out_1, out_2
+):
+    nc = tc.nc
+    with ExitStack() as ctx:
+        sb = ctx.enter_context(tc.tile_pool(name="sb", bufs=1))
+        wide_ps = ctx.enter_context(tc.psum_pool(name="wide_ps", bufs=4))
+        narrow_ps = ctx.enter_context(tc.psum_pool(name="narrow_ps", bufs=1))
+
+        def tile(name, shape, dtype, tag=None):
+            return sb.tile(shape, dtype, name=name, tag=tag or name, align_bytes=64)
+
+        key_list = tile("key_list", [P, I // 16], U16)
+        wide_list = tile("wide_list", [P, J // 16], U16)
+        user_list = tile("user_list", [P, J // 16], U16)
+        run_list = tile("run_list", [P, N // 16], U16)
+        pool_words = tile("pool_words", [P, T], U16)
+        pool_scales = tile("pool_scales", [P, T], U8)
+        chunks = range(U // CHUNK)
+        places = range(PACK)
+        notes_f32 = [tile(f"notes_f32_{h}", [P, PACK, CHUNK], F32) for h in chunks]
+        users_f32 = [tile(f"users_f32_{t}", [P, Z], F32) for t in places]
+        old_f32 = tile("old_f32", [P, PACK, M], F32)
+        placed = [tile(f"placed_{t}", [P, M], F32) for t in places]
+
+        nc.vector.memset(pool_scales[:].bitcast(I32), 0)
+        for t in places:
+            nc.vector.memset(placed[t][:], 0.0)
+
+        notes_rows = notes.rearrange("(p t) u -> p t u", t=PACK)
+        users_rows = users2.rearrange("(p t) z -> p t z", t=PACK)
+        nc.sync.dma_start(pool_words[:].bitcast(I32), keys_words[0].bitcast(I32))
+        nc.sync.dma_start(key_list[:], offs)
+        nc.sync.dma_start(user_list[:], offs3)
+        for q in range(4):
+            nc.sync.dma_start(
+                pool_scales[32 * q : 32 * q + 4, :].bitcast(I32),
+                keys_scales[0, 4 * q : 4 * q + 4, :].bitcast(I32),
+            )
+        nc.sync.dma_start(notes_f32[0][:], notes_rows[:, :, :CHUNK])
+        nc.sync.dma_start(wide_list[:], offs2)
+        nc.sync.dma_start(run_list[:], offs4)
+        for h in chunks[1:]:
+            nc.sync.dma_start(notes_f32[h][:], notes_rows[:, :, h * CHUNK : (h + 1) * CHUNK])
+        for t in places:
+            nc.sync.dma_start(users_f32[t][:], users_rows[:, t, :])
+        nc.sync.dma_start(old_f32[:], old.rearrange("(p t) m -> p t m", t=PACK))
+
+        listed_words = tile("listed_words", [P, I], U16)
+        key_words = tile("key_words", [P, I], U16)
+        key_scales = tile("key_scales", [P, I], U8)
+        nc.vector.tensor_copy(listed_words[:], pool_words[:].indirect(key_list[:]))
+        nc.vector.tensor_copy(
+            key_scales[:].rearrange("p (t s) -> p s t", t=PACK), pool_scales[:].indirect(key_list[:])
+        )
+        nc.vector.tensor_copy(
+            key_words[:].rearrange("p (t s) -> p t s", t=PACK),
+            listed_words[:].rearrange("p (s t) -> p t s", t=PACK),
+        )
+
+        def product(bank, t, codes, scales):
+            rows = slice(t * P, (t + 1) * P)
+            nc.tensor.matmul_mx(
+                out=bank,
+                lhsT=key_words[:, rows].bitcast(FP4X4),
+                lhsT_scale=key_scales[:, rows],
+                rhs=codes[:].bitcast(FP8X4),
+                rhs_scale=scales[:],
+                start=True,
+                stop=True,
+            )
+
+        wide = tile("wide", [P, PACK, U], F32)
+        wide_listed = {}
+        notes_codes = [tile(f"notes_codes_{h}", [P, CHUNK], U32) for h in chunks]
+        notes_scales = [tile(f"notes_scales_{h}", [P, CHUNK], U8) for h in chunks]
+
+        def wide_chunk(t0, count, h):
+            bank = wide_ps.tile([P, count, CHUNK], F32, name="wide_bank")
+            for e in range(count):
+                product(bank[:, e, :], t0 + e, notes_codes[h], notes_scales[h])
+            nc.scalar.copy(wide[:, t0 : t0 + count, h * CHUNK : (h + 1) * CHUNK], bank[:])
+
+        def wide_lookup(t, listed):
+            wide_listed[t] = listed
+            nc.scalar.activation(listed, wide[:, t, :].indirect(wide_list[:]), COPY)
+
+        def runs(values):
+            return values.rearrange("p (n r) -> p n r", r=RUN)
+
+        for h in chunks:
+            notes_bf16 = tile(f"notes_bf16_{h}", [P, CHUNK, PACK], BF16, tag="staged" if h == chunks[-1] else None)
+            interleave(nc.scalar.copy if h < 2 else nc.vector.tensor_copy, notes_bf16, notes_f32[h], 0, CHUNK)
+            quantize(nc, notes_codes[h], notes_scales[h], notes_bf16)
+        for h in chunks[:-1]:
+            for t in places[::2]:
+                wide_chunk(t, 2, h)
+
+        users_listed = tile("users_listed", [P, PACK, J], BF16, tag="staged")
+        users_bf16 = tile("users_bf16", [P, J, PACK], BF16)
+        users_codes = tile("users_codes", [P, J], U32)
+        users_scales = tile("users_scales", [P, J], U8)
+        early = tile("early", [P, J], F32)
+        wide_chunk(0, 2, chunks[-1])
+        wide_lookup(0, early[:])
+        wide_chunk(2, 2, chunks[-1])
+        for t in places[:-1]:
+            nc.vector.tensor_copy(users_listed[:, t, :], users_f32[t][:].indirect(user_list[:]))
+        last = places[-1]
+        half = J // 2
+        nc.vector.tensor_copy(users_listed[:, last, half:], users_f32[last][:].indirect(user_list[:, half // 16 :]))
+        nc.scalar.activation(users_listed[:, last, :half], users_f32[last][:].indirect(user_list[:, : half // 16]), COPY)
+        interleave(nc.scalar.copy, users_bf16, users_listed, 0, USERS_ON_SCALAR)
+        interleave(nc.vector.tensor_copy, users_bf16, users_listed, USERS_ON_SCALAR, J)
+        quantize(nc, users_codes, users_scales, users_bf16)
+        late = tile("late", [P, PACK - 1, J], F32, tag="staged")
+        for t in places[1:]:
+            wide_lookup(t, late[:, t - 1, :])
+
+        result = tile("result", [P, PACK, M], F32)
+        out_rows = out_0.rearrange("(p t) m -> p t m", t=PACK)
+        for t in places:
+            narrow = narrow_ps.tile([P, J], F32, name=f"narrow_{t}")
+            product(narrow[:], t, users_codes, users_scales)
+            both_max = tile(f"both_max_{t}", [P, 2, N], F32)
+            run_max = tile(f"run_max_{t}", [P, N], F32)
+            nc.vector.tensor_reduce(both_max[:, 0, :], runs(wide_listed[t]), AXIS_X, MAX)
+            nc.vector.tensor_reduce(both_max[:, 1, :], runs(narrow[:]), AXIS_X, MAX)
+            nc.vector.tensor_reduce(run_max[:], both_max[:].rearrange("p e n -> p n e"), AXIS_X, MAX)
+            nc.scalar.activation(placed[t][:].indirect(run_list[:]), run_max[:], COPY)
+            nc.vector.tensor_tensor(result[:, t, :], old_f32[:, t, :], placed[t][:], ADD)
+            nc.sync.dma_start(out_rows[:, t, :], result[:, t, :])
+
+        result_bf16 = tile("result_bf16", [P, M, PACK], BF16)
+        result_codes = tile("result_codes", [P, M], U32)
+        result_scales = tile("result_scales", [P, M], U8)
+        interleave(nc.scalar.copy, result_bf16, result, 0, RESULT_ON_SCALAR)
+        interleave(nc.vector.tensor_copy, result_bf16, result, RESULT_ON_SCALAR, M)
+        quantize(nc, result_codes, result_scales, result_bf16)
+        nc.sync.dma_start(out_1[0].rearrange("p c r -> p (c r)").bitcast(I32), result_codes[:].bitcast(I32))
+        for q in range(4):
+            engine = nc.sync if q % 2 else nc.scalar
+            engine.dma_start(
+                out_2[0, 4 * q : 4 * q + 4, :].bitcast(I32),
+                result_scales[32 * q : 32 * q + 4, :].bitcast(I32),
+            )

@@ -24,21 +24,20 @@ BANK = 512
 RUN = J // N
 LINE = 4
 CHUNK = 256
-USERS_ON_SCALAR = 192
-RESULT_ON_SCALAR = 192
+HALF = 256
 
 
-def interleave(copy, words, planes, first, last):
+def interleave(copy, words, planes):
     copy(
-        out=words[:, first:last, :].rearrange("p (c i) t -> p c t i", i=LINE),
-        in_=planes[:, :, first:last].rearrange("p t (c i) -> p c t i", i=LINE),
+        out=words.rearrange("p (c i) t -> p c t i", i=LINE),
+        in_=planes.rearrange("p t (c i) -> p c t i", i=LINE),
     )
 
 
 def quantize(nc, codes, scales, words):
     nc.vector.quantize_mx(
-        out=codes[:].bitcast(FP8X4),
-        scales=scales[:],
+        out=codes.bitcast(FP8X4),
+        scales=scales,
         in_=words[:].rearrange("p c t -> p (c t)"),
     )
 
@@ -135,29 +134,28 @@ def tile_attend_tab_wideandown_runsput_pl_kernel(
 
         for h in chunks:
             notes_bf16 = tile(f"notes_bf16_{h}", [P, CHUNK, PACK], BF16, tag="staged" if h == chunks[-1] else None)
-            interleave(nc.scalar.copy if h < 2 else nc.vector.tensor_copy, notes_bf16, notes_f32[h], 0, CHUNK)
-            quantize(nc, notes_codes[h], notes_scales[h], notes_bf16)
+            interleave(nc.scalar.copy if h < 2 else nc.vector.tensor_copy, notes_bf16[:], notes_f32[h][:])
+            quantize(nc, notes_codes[h][:], notes_scales[h][:], notes_bf16)
         for h in chunks[:-1]:
             for t in places[::2]:
                 wide_chunk(t, 2, h)
 
         users_listed = tile("users_listed", [P, PACK, J], BF16, tag="staged")
-        users_bf16 = tile("users_bf16", [P, J, PACK], BF16)
-        users_codes = tile("users_codes", [P, J], U32)
-        users_scales = tile("users_scales", [P, J], U8)
+        users_bf16 = [tile(f"users_bf16_{e}", [P, HALF, PACK], BF16) for e in range(2)]
+        users_codes = [tile(f"users_codes_{e}", [P, HALF], U32) for e in range(2)]
+        users_scales = [tile(f"users_scales_{e}", [P, HALF], U8) for e in range(2)]
         early = tile("early", [P, J], F32)
         wide_chunk(0, 2, chunks[-1])
         wide_lookup(0, early[:])
         wide_chunk(2, 2, chunks[-1])
+        last = places[-1]
         for t in places[:-1]:
             nc.vector.tensor_copy(users_listed[:, t, :], users_f32[t][:].indirect(user_list[:]))
-        last = places[-1]
-        half = J // 2
-        nc.vector.tensor_copy(users_listed[:, last, half:], users_f32[last][:].indirect(user_list[:, half // 16 :]))
-        nc.scalar.activation(users_listed[:, last, :half], users_f32[last][:].indirect(user_list[:, : half // 16]), COPY)
-        interleave(nc.scalar.copy, users_bf16, users_listed, 0, USERS_ON_SCALAR)
-        interleave(nc.vector.tensor_copy, users_bf16, users_listed, USERS_ON_SCALAR, J)
-        quantize(nc, users_codes, users_scales, users_bf16)
+        nc.vector.tensor_copy(users_listed[:, last, :HALF], users_f32[last][:].indirect(user_list[:, : HALF // 16]))
+        nc.scalar.activation(users_listed[:, last, HALF:], users_f32[last][:].indirect(user_list[:, HALF // 16 :]), COPY)
+        for e, copy in enumerate((nc.vector.tensor_copy, nc.scalar.copy)):
+            interleave(copy, users_bf16[e][:], users_listed[:, :, e * HALF : (e + 1) * HALF])
+            quantize(nc, users_codes[e][:], users_scales[e][:], users_bf16[e])
         late = tile("late", [P, PACK - 1, J], F32, tag="staged")
         for t in places[1:]:
             wide_lookup(t, late[:, t - 1, :])
@@ -166,23 +164,32 @@ def tile_attend_tab_wideandown_runsput_pl_kernel(
         out_rows = out_0.rearrange("(p t) m -> p t m", t=PACK)
         for t in places:
             narrow = narrow_ps.tile([P, J], F32, name=f"narrow_{t}")
-            product(narrow[:], t, users_codes, users_scales)
-            both_max = tile(f"both_max_{t}", [P, 2, N], F32)
+            for e in range(2):
+                product(narrow[:, e * HALF : (e + 1) * HALF], t, users_codes[e], users_scales[e])
+            table = tile(f"table_{t}", [P, J], F32)
             run_max = tile(f"run_max_{t}", [P, N], F32)
-            nc.vector.tensor_reduce(both_max[:, 0, :], runs(wide_listed[t]), AXIS_X, MAX)
-            nc.vector.tensor_reduce(both_max[:, 1, :], runs(narrow[:]), AXIS_X, MAX)
-            nc.vector.tensor_reduce(run_max[:], both_max[:].rearrange("p e n -> p n e"), AXIS_X, MAX)
+            nc.vector.tensor_tensor(table[:], narrow[:], wide_listed[t], MAX)
+            nc.vector.tensor_reduce(run_max[:], runs(table[:]), AXIS_X, MAX)
             nc.scalar.activation(placed[t][:].indirect(run_list[:]), run_max[:], COPY)
-            nc.vector.tensor_tensor(result[:, t, :], old_f32[:, t, :], placed[t][:], ADD)
+            if t < 2:
+                nc.gpsimd.tensor_tensor(result[:, t, :], old_f32[:, t, :], placed[t][:], ADD)
+            elif t < last:
+                nc.vector.tensor_tensor(result[:, t, :], old_f32[:, t, :], placed[t][:], ADD)
+            else:
+                for e in (1, 0):
+                    cols = slice(e * HALF, (e + 1) * HALF)
+                    nc.vector.tensor_tensor(result[:, t, cols], old_f32[:, t, cols], placed[t][:, cols], ADD)
             nc.sync.dma_start(out_rows[:, t, :], result[:, t, :])
 
-        result_bf16 = tile("result_bf16", [P, M, PACK], BF16)
         result_codes = tile("result_codes", [P, M], U32)
         result_scales = tile("result_scales", [P, M], U8)
-        interleave(nc.scalar.copy, result_bf16, result, 0, RESULT_ON_SCALAR)
-        interleave(nc.vector.tensor_copy, result_bf16, result, RESULT_ON_SCALAR, M)
-        quantize(nc, result_codes, result_scales, result_bf16)
-        nc.sync.dma_start(out_1[0].rearrange("p c r -> p (c r)").bitcast(I32), result_codes[:].bitcast(I32))
+        out_words = out_1[0].rearrange("p c r -> p (c r)").bitcast(I32)
+        for e, copy in enumerate((nc.vector.tensor_copy, nc.scalar.copy)):
+            cols = slice(e * HALF, (e + 1) * HALF)
+            result_bf16 = tile(f"result_bf16_{e}", [P, HALF, PACK], BF16)
+            interleave(copy, result_bf16[:], result[:, :, cols])
+            quantize(nc, result_codes[:, cols], result_scales[:, cols], result_bf16)
+            nc.sync.dma_start(out_words[:, cols], result_codes[:, cols].bitcast(I32))
         for q in range(4):
             engine = nc.sync if q % 2 else nc.scalar
             engine.dma_start(

@@ -20,11 +20,14 @@ AXIS_X = mybir.AxisListType.X
 
 P = 128
 PACK = 4
-BANK = 512
+GROUP = 16
 RUN = J // N
 LINE = 4
-CHUNK = 256
-HALF = 256
+WIDTH = 256
+USERS_TAIL = 128
+PLACES = range(PACK)
+CHUNKS = range(U // WIDTH)
+HALVES = (slice(0, WIDTH), slice(WIDTH, 2 * WIDTH))
 
 
 def interleave(copy, words, planes):
@@ -35,11 +38,7 @@ def interleave(copy, words, planes):
 
 
 def quantize(nc, codes, scales, words):
-    nc.vector.quantize_mx(
-        out=codes.bitcast(FP8X4),
-        scales=scales,
-        in_=words[:].rearrange("p c t -> p (c t)"),
-    )
+    nc.vector.quantize_mx(out=codes.bitcast(FP8X4), scales=scales, in_=words.rearrange("p c t -> p (c t)"))
 
 
 def tile_attend_tab_wideandown_runsput_pl_kernel(
@@ -47,47 +46,48 @@ def tile_attend_tab_wideandown_runsput_pl_kernel(
 ):
     nc = tc.nc
     with ExitStack() as ctx:
-        sb = ctx.enter_context(tc.tile_pool(name="sb", bufs=1))
-        wide_ps = ctx.enter_context(tc.psum_pool(name="wide_ps", bufs=4))
-        narrow_ps = ctx.enter_context(tc.psum_pool(name="narrow_ps", bufs=1))
+        sbuf = ctx.enter_context(tc.tile_pool(name="sbuf", bufs=1))
+        psum = ctx.enter_context(tc.psum_pool(name="psum", bufs=1))
 
         def tile(name, shape, dtype, tag=None):
-            return sb.tile(shape, dtype, name=name, tag=tag or name, align_bytes=64)
+            return sbuf.tile(shape, dtype, name=name, tag=tag or name, align_bytes=64)
 
-        key_list = tile("key_list", [P, I // 16], U16)
-        wide_list = tile("wide_list", [P, J // 16], U16)
-        user_list = tile("user_list", [P, J // 16], U16)
-        run_list = tile("run_list", [P, N // 16], U16)
+        def bank(name, shape, number):
+            return psum.tile(shape, F32, name=name, tag=f"bank_{number}")
+
+        key_list = tile("key_list", [P, I // GROUP], U16)
+        wide_list = tile("wide_list", [P, J // GROUP], U16)
+        user_list = tile("user_list", [P, J // GROUP], U16)
+        run_list = tile("run_list", [P, N // GROUP], U16)
         pool_words = tile("pool_words", [P, T], U16)
         pool_scales = tile("pool_scales", [P, T], U8)
-        chunks = range(U // CHUNK)
-        places = range(PACK)
-        notes_f32 = [tile(f"notes_f32_{h}", [P, PACK, CHUNK], F32) for h in chunks]
-        users_f32 = [tile(f"users_f32_{t}", [P, Z], F32) for t in places]
+        notes_f32 = [tile(f"notes_f32_{h}", [P, PACK, WIDTH], F32) for h in CHUNKS]
+        users_f32 = [tile(f"users_f32_{t}", [P, Z], F32) for t in PLACES]
         old_f32 = tile("old_f32", [P, PACK, M], F32)
-        placed = [tile(f"placed_{t}", [P, M], F32) for t in places]
+        placed = [tile(f"placed_{t}", [P, M], F32) for t in PLACES]
 
         nc.vector.memset(pool_scales[:].bitcast(I32), 0)
-        for t in places:
+        for t in PLACES:
             nc.vector.memset(placed[t][:], 0.0)
 
         notes_rows = notes.rearrange("(p t) u -> p t u", t=PACK)
         users_rows = users2.rearrange("(p t) z -> p t z", t=PACK)
         nc.sync.dma_start(pool_words[:].bitcast(I32), keys_words[0].bitcast(I32))
         nc.sync.dma_start(key_list[:], offs)
-        nc.sync.dma_start(user_list[:], offs3)
-        for q in range(4):
+        for q in (0, 2, 1, 3):
             nc.sync.dma_start(
                 pool_scales[32 * q : 32 * q + 4, :].bitcast(I32),
                 keys_scales[0, 4 * q : 4 * q + 4, :].bitcast(I32),
             )
-        nc.sync.dma_start(notes_f32[0][:], notes_rows[:, :, :CHUNK])
-        nc.sync.dma_start(wide_list[:], offs2)
-        nc.sync.dma_start(run_list[:], offs4)
-        for h in chunks[1:]:
-            nc.sync.dma_start(notes_f32[h][:], notes_rows[:, :, h * CHUNK : (h + 1) * CHUNK])
-        for t in places:
+        for h in CHUNKS:
+            nc.sync.dma_start(notes_f32[h][:], notes_rows[:, :, h * WIDTH : (h + 1) * WIDTH])
+        nc.sync.dma_start(user_list[:], offs3)
+        for t in PLACES[:2]:
             nc.sync.dma_start(users_f32[t][:], users_rows[:, t, :])
+        nc.sync.dma_start(wide_list[:], offs2)
+        for t in PLACES[2:]:
+            nc.sync.dma_start(users_f32[t][:], users_rows[:, t, :])
+        nc.sync.dma_start(run_list[:], offs4)
         nc.sync.dma_start(old_f32[:], old.rearrange("(p t) m -> p t m", t=PACK))
 
         listed_words = tile("listed_words", [P, I], U16)
@@ -102,97 +102,113 @@ def tile_attend_tab_wideandown_runsput_pl_kernel(
             listed_words[:].rearrange("p (s t) -> p t s", t=PACK),
         )
 
-        def product(bank, t, codes, scales):
+        def product(out, t, codes, scales):
             rows = slice(t * P, (t + 1) * P)
             nc.tensor.matmul_mx(
-                out=bank,
+                out=out,
                 lhsT=key_words[:, rows].bitcast(FP4X4),
                 lhsT_scale=key_scales[:, rows],
-                rhs=codes[:].bitcast(FP8X4),
-                rhs_scale=scales[:],
+                rhs=codes.bitcast(FP8X4),
+                rhs_scale=scales,
                 start=True,
                 stop=True,
             )
 
+        notes_codes = [tile(f"notes_codes_{h}", [P, WIDTH], U32) for h in CHUNKS]
+        notes_scales = [tile(f"notes_scales_{h}", [P, WIDTH], U8) for h in CHUNKS]
+        for h, tag in ((0, None), (1, "staged")):
+            notes_bf16 = tile(f"notes_bf16_{h}", [P, WIDTH, PACK], BF16, tag=tag)
+            interleave(nc.scalar.copy, notes_bf16[:], notes_f32[h][:])
+            quantize(nc, notes_codes[h][:], notes_scales[h][:], notes_bf16[:])
+        last_notes_bf16 = tile("last_notes_bf16", [P, 2, WIDTH, PACK], BF16, tag="staged")
+        for e, h in enumerate(CHUNKS[2:]):
+            interleave(nc.vector.tensor_copy, last_notes_bf16[:, e], notes_f32[h][:])
+            quantize(nc, notes_codes[h][:], notes_scales[h][:], last_notes_bf16[:, e])
+
         wide = tile("wide", [P, PACK, U], F32)
-        wide_listed = {}
-        notes_codes = [tile(f"notes_codes_{h}", [P, CHUNK], U32) for h in chunks]
-        notes_scales = [tile(f"notes_scales_{h}", [P, CHUNK], U8) for h in chunks]
 
-        def wide_chunk(t0, count, h):
-            bank = wide_ps.tile([P, count, CHUNK], F32, name="wide_bank")
-            for e in range(count):
-                product(bank[:, e, :], t0 + e, notes_codes[h], notes_scales[h])
-            nc.scalar.copy(wide[:, t0 : t0 + count, h * CHUNK : (h + 1) * CHUNK], bank[:])
+        def wide_pair(pair, h):
+            sums = bank(f"wide_{h}_{pair}", [P, 2, WIDTH], 2 * h + pair)
+            for e in range(2):
+                product(sums[:, e, :], 2 * pair + e, notes_codes[h][:], notes_scales[h][:])
+            nc.scalar.copy(wide[:, 2 * pair : 2 * pair + 2, h * WIDTH : (h + 1) * WIDTH], sums[:])
 
-        def wide_lookup(t, listed):
-            wide_listed[t] = listed
+        def look_up(t, listed):
             nc.scalar.activation(listed, wide[:, t, :].indirect(wide_list[:]), COPY)
+            return listed
 
-        def runs(values):
-            return values.rearrange("p (n r) -> p n r", r=RUN)
-
-        for h in chunks:
-            notes_bf16 = tile(f"notes_bf16_{h}", [P, CHUNK, PACK], BF16, tag="staged" if h == chunks[-1] else None)
-            interleave(nc.scalar.copy if h < 2 else nc.vector.tensor_copy, notes_bf16[:], notes_f32[h][:])
-            quantize(nc, notes_codes[h][:], notes_scales[h][:], notes_bf16)
-        for h in chunks[:-1]:
-            for t in places[::2]:
-                wide_chunk(t, 2, h)
+        for h in CHUNKS[:-1]:
+            for pair in range(2):
+                wide_pair(pair, h)
+        wide_pair(0, CHUNKS[-1])
+        first_listed = tile("first_listed", [P, J], F32)
+        wide_listed = [look_up(0, first_listed[:])]
+        wide_pair(1, CHUNKS[-1])
 
         users_listed = tile("users_listed", [P, PACK, J], BF16, tag="staged")
-        users_bf16 = [tile(f"users_bf16_{e}", [P, HALF, PACK], BF16) for e in range(2)]
-        users_codes = [tile(f"users_codes_{e}", [P, HALF], U32) for e in range(2)]
-        users_scales = [tile(f"users_scales_{e}", [P, HALF], U8) for e in range(2)]
-        early = tile("early", [P, J], F32)
-        wide_chunk(0, 2, chunks[-1])
-        wide_lookup(0, early[:])
-        wide_chunk(2, 2, chunks[-1])
-        last = places[-1]
-        for t in places[:-1]:
+        users_bf16 = tile("users_bf16", [P, J, PACK], BF16)
+        users_codes = tile("users_codes", [P, J], U32)
+        users_scales = tile("users_scales", [P, J], U8)
+        last = PLACES[-1]
+        for t in PLACES[:-1]:
             nc.vector.tensor_copy(users_listed[:, t, :], users_f32[t][:].indirect(user_list[:]))
-        nc.vector.tensor_copy(users_listed[:, last, :HALF], users_f32[last][:].indirect(user_list[:, : HALF // 16]))
-        nc.scalar.activation(users_listed[:, last, HALF:], users_f32[last][:].indirect(user_list[:, HALF // 16 :]), COPY)
-        for e, copy in enumerate((nc.vector.tensor_copy, nc.scalar.copy)):
-            interleave(copy, users_bf16[e][:], users_listed[:, :, e * HALF : (e + 1) * HALF])
-            quantize(nc, users_codes[e][:], users_scales[e][:], users_bf16[e])
-        late = tile("late", [P, PACK - 1, J], F32, tag="staged")
-        for t in places[1:]:
-            wide_lookup(t, late[:, t - 1, :])
+        nc.vector.tensor_copy(
+            users_listed[:, last, HALVES[0]], users_f32[last][:].indirect(user_list[:, : WIDTH // GROUP])
+        )
+        nc.scalar.activation(
+            users_listed[:, last, HALVES[1]], users_f32[last][:].indirect(user_list[:, WIDTH // GROUP :]), COPY
+        )
+        for copy, cols in (
+            (nc.vector.tensor_copy, HALVES[0]),
+            (nc.vector.tensor_copy, slice(WIDTH, J - USERS_TAIL)),
+            (nc.scalar.copy, slice(J - USERS_TAIL, J)),
+        ):
+            interleave(copy, users_bf16[:, cols, :], users_listed[:, :, cols])
+        for cols in HALVES:
+            quantize(nc, users_codes[:, cols], users_scales[:, cols], users_bf16[:, cols, :])
+        later_listed = tile("later_listed", [P, PACK - 1, J], F32, tag="staged")
+        wide_listed.extend(look_up(t, later_listed[:, t - 1, :]) for t in PLACES[1:])
+
+        def run_maxima(t, cols, narrow, run_max):
+            table = tile(f"table_{t}_{cols.start}", [P, cols.stop - cols.start], F32)
+            nc.vector.tensor_tensor(table[:], narrow, wide_listed[t][:, cols], MAX)
+            nc.vector.tensor_reduce(
+                run_max[:, cols.start // RUN : cols.stop // RUN],
+                table[:].rearrange("p (n r) -> p n r", r=RUN),
+                AXIS_X,
+                MAX,
+            )
 
         result = tile("result", [P, PACK, M], F32)
         out_rows = out_0.rearrange("(p t) m -> p t m", t=PACK)
-        for t in places:
-            narrow = narrow_ps.tile([P, J], F32, name=f"narrow_{t}")
-            for e in range(2):
-                product(narrow[:, e * HALF : (e + 1) * HALF], t, users_codes[e], users_scales[e])
-            table = tile(f"table_{t}", [P, J], F32)
+        for t in PLACES:
             run_max = tile(f"run_max_{t}", [P, N], F32)
-            nc.vector.tensor_tensor(table[:], narrow[:], wide_listed[t], MAX)
-            nc.vector.tensor_reduce(run_max[:], runs(table[:]), AXIS_X, MAX)
+            if t == 0:
+                for e, cols in enumerate(HALVES):
+                    narrow = bank(f"narrow_0_{e}", [P, WIDTH], PACK * e)
+                    product(narrow[:], t, users_codes[:, cols], users_scales[:, cols])
+                    run_maxima(t, cols, narrow[:], run_max)
+            else:
+                narrow = bank(f"narrow_{t}", [P, J], t)
+                for cols in HALVES:
+                    product(narrow[:, cols], t, users_codes[:, cols], users_scales[:, cols])
+                run_maxima(t, slice(0, J), narrow[:], run_max)
             nc.scalar.activation(placed[t][:].indirect(run_list[:]), run_max[:], COPY)
             if t < 2:
                 nc.gpsimd.tensor_tensor(result[:, t, :], old_f32[:, t, :], placed[t][:], ADD)
-            elif t < last:
-                nc.vector.tensor_tensor(result[:, t, :], old_f32[:, t, :], placed[t][:], ADD)
             else:
-                for e in (1, 0):
-                    cols = slice(e * HALF, (e + 1) * HALF)
+                for cols in HALVES if t == last else (slice(0, M),):
                     nc.vector.tensor_tensor(result[:, t, cols], old_f32[:, t, cols], placed[t][:, cols], ADD)
             nc.sync.dma_start(out_rows[:, t, :], result[:, t, :])
 
         result_codes = tile("result_codes", [P, M], U32)
         result_scales = tile("result_scales", [P, M], U8)
         out_words = out_1[0].rearrange("p c r -> p (c r)").bitcast(I32)
-        for e, copy in enumerate((nc.vector.tensor_copy, nc.scalar.copy)):
-            cols = slice(e * HALF, (e + 1) * HALF)
-            result_bf16 = tile(f"result_bf16_{e}", [P, HALF, PACK], BF16)
+        for copy, cols in zip((nc.vector.tensor_copy, nc.scalar.copy), HALVES):
+            result_bf16 = tile(f"result_bf16_{cols.start}", [P, WIDTH, PACK], BF16)
             interleave(copy, result_bf16[:], result[:, :, cols])
-            quantize(nc, result_codes[:, cols], result_scales[:, cols], result_bf16)
+            quantize(nc, result_codes[:, cols], result_scales[:, cols], result_bf16[:])
             nc.sync.dma_start(out_words[:, cols], result_codes[:, cols].bitcast(I32))
-        for q in range(4):
-            engine = nc.sync if q % 2 else nc.scalar
-            engine.dma_start(
-                out_2[0, 4 * q : 4 * q + 4, :].bitcast(I32),
-                result_scales[32 * q : 32 * q + 4, :].bitcast(I32),
-            )
+        for r in range(4):
+            queue = nc.sync if r % 2 else nc.scalar
+            queue.dma_start(out_2[0, r::4, :].bitcast(I32), result_scales[r::32, :].bitcast(I32))

@@ -24,7 +24,6 @@ GROUP = 16
 RUN = J // N
 LINE = 4
 WIDTH = 256
-USERS_TAIL = 128
 PLACES = range(PACK)
 CHUNKS = range(U // WIDTH)
 HALVES = (slice(0, WIDTH), slice(WIDTH, 2 * WIDTH))
@@ -74,18 +73,13 @@ def tile_attend_tab_wideandown_runsput_pl_kernel(
         users_rows = users2.rearrange("(p t) z -> p t z", t=PACK)
         nc.sync.dma_start(pool_words[:].bitcast(I32), keys_words[0].bitcast(I32))
         nc.sync.dma_start(key_list[:], offs)
-        for q in (0, 2, 1, 3):
-            nc.sync.dma_start(
-                pool_scales[32 * q : 32 * q + 4, :].bitcast(I32),
-                keys_scales[0, 4 * q : 4 * q + 4, :].bitcast(I32),
-            )
+        nc.sync.dma_start(user_list[:], offs3)
+        for r in range(4):
+            nc.sync.dma_start(pool_scales[r::32, :].bitcast(I32), keys_scales[0, r::4, :].bitcast(I32))
         for h in CHUNKS:
             nc.sync.dma_start(notes_f32[h][:], notes_rows[:, :, h * WIDTH : (h + 1) * WIDTH])
-        nc.sync.dma_start(user_list[:], offs3)
-        for t in PLACES[:2]:
-            nc.sync.dma_start(users_f32[t][:], users_rows[:, t, :])
         nc.sync.dma_start(wide_list[:], offs2)
-        for t in PLACES[2:]:
+        for t in PLACES:
             nc.sync.dma_start(users_f32[t][:], users_rows[:, t, :])
         nc.sync.dma_start(run_list[:], offs4)
         nc.sync.dma_start(old_f32[:], old.rearrange("(p t) m -> p t m", t=PACK))
@@ -145,10 +139,10 @@ def tile_attend_tab_wideandown_runsput_pl_kernel(
         wide_listed = [look_up(0, first_listed[:])]
         wide_pair(1, CHUNKS[-1])
 
+        half_copies = (nc.vector.tensor_copy, nc.scalar.copy)
         users_listed = tile("users_listed", [P, PACK, J], BF16, tag="staged")
-        users_bf16 = tile("users_bf16", [P, J, PACK], BF16)
-        users_codes = tile("users_codes", [P, J], U32)
-        users_scales = tile("users_scales", [P, J], U8)
+        users_codes = [tile(f"users_codes_{e}", [P, WIDTH], U32) for e in range(2)]
+        users_scales = [tile(f"users_scales_{e}", [P, WIDTH], U8) for e in range(2)]
         last = PLACES[-1]
         for t in PLACES[:-1]:
             nc.vector.tensor_copy(users_listed[:, t, :], users_f32[t][:].indirect(user_list[:]))
@@ -158,57 +152,42 @@ def tile_attend_tab_wideandown_runsput_pl_kernel(
         nc.scalar.activation(
             users_listed[:, last, HALVES[1]], users_f32[last][:].indirect(user_list[:, WIDTH // GROUP :]), COPY
         )
-        for copy, cols in (
-            (nc.vector.tensor_copy, HALVES[0]),
-            (nc.vector.tensor_copy, slice(WIDTH, J - USERS_TAIL)),
-            (nc.scalar.copy, slice(J - USERS_TAIL, J)),
-        ):
-            interleave(copy, users_bf16[:, cols, :], users_listed[:, :, cols])
-        for cols in HALVES:
-            quantize(nc, users_codes[:, cols], users_scales[:, cols], users_bf16[:, cols, :])
+        for e, copy in enumerate(half_copies):
+            users_bf16 = tile(f"users_bf16_{e}", [P, WIDTH, PACK], BF16)
+            interleave(copy, users_bf16[:], users_listed[:, :, HALVES[e]])
+            quantize(nc, users_codes[e][:], users_scales[e][:], users_bf16[:])
         later_listed = tile("later_listed", [P, PACK - 1, J], F32, tag="staged")
         wide_listed.extend(look_up(t, later_listed[:, t - 1, :]) for t in PLACES[1:])
-
-        def run_maxima(t, cols, narrow, run_max):
-            table = tile(f"table_{t}_{cols.start}", [P, cols.stop - cols.start], F32)
-            nc.vector.tensor_tensor(table[:], narrow, wide_listed[t][:, cols], MAX)
-            nc.vector.tensor_reduce(
-                run_max[:, cols.start // RUN : cols.stop // RUN],
-                table[:].rearrange("p (n r) -> p n r", r=RUN),
-                AXIS_X,
-                MAX,
-            )
 
         result = tile("result", [P, PACK, M], F32)
         out_rows = out_0.rearrange("(p t) m -> p t m", t=PACK)
         for t in PLACES:
+            narrow = bank(f"narrow_{t}", [P, J], t)
+            for e, cols in enumerate(HALVES):
+                product(narrow[:, cols], t, users_codes[e][:], users_scales[e][:])
+            table = tile(f"table_{t}", [P, J], F32)
             run_max = tile(f"run_max_{t}", [P, N], F32)
-            if t == 0:
-                for e, cols in enumerate(HALVES):
-                    narrow = bank(f"narrow_0_{e}", [P, WIDTH], PACK * e)
-                    product(narrow[:], t, users_codes[:, cols], users_scales[:, cols])
-                    run_maxima(t, cols, narrow[:], run_max)
-            else:
-                narrow = bank(f"narrow_{t}", [P, J], t)
-                for cols in HALVES:
-                    product(narrow[:, cols], t, users_codes[:, cols], users_scales[:, cols])
-                run_maxima(t, slice(0, J), narrow[:], run_max)
+            nc.vector.tensor_tensor(table[:], narrow[:], wide_listed[t], MAX)
+            nc.vector.tensor_reduce(run_max[:], table[:].rearrange("p (n r) -> p n r", r=RUN), AXIS_X, MAX)
             nc.scalar.activation(placed[t][:].indirect(run_list[:]), run_max[:], COPY)
             if t < 2:
                 nc.gpsimd.tensor_tensor(result[:, t, :], old_f32[:, t, :], placed[t][:], ADD)
             else:
-                for cols in HALVES if t == last else (slice(0, M),):
+                for cols in HALVES[::-1] if t == last else (slice(0, M),):
                     nc.vector.tensor_tensor(result[:, t, cols], old_f32[:, t, cols], placed[t][:, cols], ADD)
             nc.sync.dma_start(out_rows[:, t, :], result[:, t, :])
 
         result_codes = tile("result_codes", [P, M], U32)
         result_scales = tile("result_scales", [P, M], U8)
         out_words = out_1[0].rearrange("p c r -> p (c r)").bitcast(I32)
-        for copy, cols in zip((nc.vector.tensor_copy, nc.scalar.copy), HALVES):
+        for copy, cols in zip(half_copies, HALVES):
             result_bf16 = tile(f"result_bf16_{cols.start}", [P, WIDTH, PACK], BF16)
             interleave(copy, result_bf16[:], result[:, :, cols])
             quantize(nc, result_codes[:, cols], result_scales[:, cols], result_bf16[:])
             nc.sync.dma_start(out_words[:, cols], result_codes[:, cols].bitcast(I32))
-        for r in range(4):
-            queue = nc.sync if r % 2 else nc.scalar
-            queue.dma_start(out_2[0, r::4, :].bitcast(I32), result_scales[r::32, :].bitcast(I32))
+        for q in range(4):
+            queue = nc.sync if q % 2 else nc.scalar
+            queue.dma_start(
+                out_2[0, 4 * q : 4 * q + 4, :].bitcast(I32),
+                result_scales[32 * q : 32 * q + 4, :].bitcast(I32),
+            )

from contextlib import ExitStack

import concourse.mybir as mybir

D, T, I, J, U, Z, M, N = 512, 2048, 512, 512, 1024, 1024, 512, 64
FLOPS = 2 * D * I * (U + J)

F32 = mybir.dt.float32
BF16 = mybir.dt.bfloat16
I32 = mybir.dt.int32
U32 = mybir.dt.uint32
U16 = mybir.dt.uint16
U8 = mybir.dt.uint8
FP8X4 = mybir.dt.float8_e4m3fn_x4
FP4X4 = mybir.dt.float4_e2m1fn_x4
COPY = mybir.ActivationFunctionType.Copy
MAX = mybir.AluOpType.max
ADD = mybir.AluOpType.add
AXIS_X = mybir.AxisListType.X

P = 128
PACK = 4
GROUP = 16
RUN = J // N
LINE = 4
WIDTH = 256
PLACES = range(PACK)
CHUNKS = range(U // WIDTH)
HALVES = (slice(0, WIDTH), slice(WIDTH, 2 * WIDTH))


def interleave(copy, words, planes):
    copy(
        out=words.rearrange("p (c i) t -> p c t i", i=LINE),
        in_=planes.rearrange("p t (c i) -> p c t i", i=LINE),
    )


def quantize(nc, codes, scales, words):
    nc.vector.quantize_mx(out=codes.bitcast(FP8X4), scales=scales, in_=words.rearrange("p c t -> p (c t)"))


def tile_attend_tab_wideandown_runsput_pl_kernel(
    tc, keys_words, keys_scales, notes, users2, old, offs, offs2, offs3, offs4, out_0, out_1, out_2
):
    nc = tc.nc
    with ExitStack() as ctx:
        sbuf = ctx.enter_context(tc.tile_pool(name="sbuf", bufs=1))
        psum = ctx.enter_context(tc.psum_pool(name="psum", bufs=1))

        def tile(name, shape, dtype, tag=None):
            return sbuf.tile(shape, dtype, name=name, tag=tag or name, align_bytes=64)

        def bank(name, shape, number):
            return psum.tile(shape, F32, name=name, tag=f"bank_{number}")

        key_list = tile("key_list", [P, I // GROUP], U16)
        wide_list = tile("wide_list", [P, J // GROUP], U16)
        user_list = tile("user_list", [P, J // GROUP], U16)
        run_list = tile("run_list", [P, N // GROUP], U16)
        pool_words = tile("pool_words", [P, T], U16)
        pool_scales = tile("pool_scales", [P, T], U8)
        notes_f32 = [tile(f"notes_f32_{h}", [P, PACK, WIDTH], F32) for h in CHUNKS]
        users_f32 = [tile(f"users_f32_{t}", [P, Z], F32) for t in PLACES]
        old_f32 = tile("old_f32", [P, PACK, M], F32)
        placed = [tile(f"placed_{t}", [P, M], F32) for t in PLACES]

        nc.vector.memset(pool_scales[:].bitcast(I32), 0)
        for t in PLACES:
            nc.vector.memset(placed[t][:], 0.0)

        notes_rows = notes.rearrange("(p t) u -> p t u", t=PACK)
        users_rows = users2.rearrange("(p t) z -> p t z", t=PACK)
        nc.sync.dma_start(pool_words[:].bitcast(I32), keys_words[0].bitcast(I32))
        nc.sync.dma_start(key_list[:], offs)
        nc.sync.dma_start(user_list[:], offs3)
        for r in range(4):
            nc.sync.dma_start(pool_scales[r::32, :].bitcast(I32), keys_scales[0, r::4, :].bitcast(I32))
        for h in CHUNKS:
            nc.sync.dma_start(notes_f32[h][:], notes_rows[:, :, h * WIDTH : (h + 1) * WIDTH])
        nc.sync.dma_start(wide_list[:], offs2)
        for t in PLACES:
            nc.sync.dma_start(users_f32[t][:], users_rows[:, t, :])
        nc.sync.dma_start(run_list[:], offs4)
        nc.sync.dma_start(old_f32[:], old.rearrange("(p t) m -> p t m", t=PACK))

        listed_words = tile("listed_words", [P, I], U16)
        key_words = tile("key_words", [P, I], U16)
        key_scales = tile("key_scales", [P, I], U8)
        nc.vector.tensor_copy(listed_words[:], pool_words[:].indirect(key_list[:]))
        nc.vector.tensor_copy(
            key_scales[:].rearrange("p (t s) -> p s t", t=PACK), pool_scales[:].indirect(key_list[:])
        )
        nc.vector.tensor_copy(
            key_words[:].rearrange("p (t s) -> p t s", t=PACK),
            listed_words[:].rearrange("p (s t) -> p t s", t=PACK),
        )

        def product(out, t, codes, scales):
            rows = slice(t * P, (t + 1) * P)
            nc.tensor.matmul_mx(
                out=out,
                lhsT=key_words[:, rows].bitcast(FP4X4),
                lhsT_scale=key_scales[:, rows],
                rhs=codes.bitcast(FP8X4),
                rhs_scale=scales,
                start=True,
                stop=True,
            )

        notes_codes = [tile(f"notes_codes_{h}", [P, WIDTH], U32) for h in CHUNKS]
        notes_scales = [tile(f"notes_scales_{h}", [P, WIDTH], U8) for h in CHUNKS]
        for h, tag in ((0, None), (1, "staged")):
            notes_bf16 = tile(f"notes_bf16_{h}", [P, WIDTH, PACK], BF16, tag=tag)
            interleave(nc.scalar.copy, notes_bf16[:], notes_f32[h][:])
            quantize(nc, notes_codes[h][:], notes_scales[h][:], notes_bf16[:])
        last_notes_bf16 = tile("last_notes_bf16", [P, 2, WIDTH, PACK], BF16, tag="staged")
        for e, h in enumerate(CHUNKS[2:]):
            interleave(nc.vector.tensor_copy, last_notes_bf16[:, e], notes_f32[h][:])
            quantize(nc, notes_codes[h][:], notes_scales[h][:], last_notes_bf16[:, e])

        wide = tile("wide", [P, PACK, U], F32)

        def wide_pair(pair, h):
            sums = bank(f"wide_{h}_{pair}", [P, 2, WIDTH], 2 * h + pair)
            for e in range(2):
                product(sums[:, e, :], 2 * pair + e, notes_codes[h][:], notes_scales[h][:])
            nc.scalar.copy(wide[:, 2 * pair : 2 * pair + 2, h * WIDTH : (h + 1) * WIDTH], sums[:])

        def look_up(t, listed):
            nc.scalar.activation(listed, wide[:, t, :].indirect(wide_list[:]), COPY)
            return listed

        for h in CHUNKS[:-1]:
            for pair in range(2):
                wide_pair(pair, h)
        wide_pair(0, CHUNKS[-1])
        first_listed = tile("first_listed", [P, J], F32)
        wide_listed = [look_up(0, first_listed[:])]
        wide_pair(1, CHUNKS[-1])

        half_copies = (nc.vector.tensor_copy, nc.scalar.copy)
        users_listed = tile("users_listed", [P, PACK, J], BF16, tag="staged")
        users_codes = [tile(f"users_codes_{e}", [P, WIDTH], U32) for e in range(2)]
        users_scales = [tile(f"users_scales_{e}", [P, WIDTH], U8) for e in range(2)]
        last = PLACES[-1]
        for t in PLACES[:-1]:
            nc.vector.tensor_copy(users_listed[:, t, :], users_f32[t][:].indirect(user_list[:]))
        nc.vector.tensor_copy(
            users_listed[:, last, HALVES[0]], users_f32[last][:].indirect(user_list[:, : WIDTH // GROUP])
        )
        nc.scalar.activation(
            users_listed[:, last, HALVES[1]], users_f32[last][:].indirect(user_list[:, WIDTH // GROUP :]), COPY
        )
        for e, copy in enumerate(half_copies):
            users_bf16 = tile(f"users_bf16_{e}", [P, WIDTH, PACK], BF16)
            interleave(copy, users_bf16[:], users_listed[:, :, HALVES[e]])
            quantize(nc, users_codes[e][:], users_scales[e][:], users_bf16[:])
        later_listed = tile("later_listed", [P, PACK - 1, J], F32, tag="staged")
        wide_listed.extend(look_up(t, later_listed[:, t - 1, :]) for t in PLACES[1:])

        result = tile("result", [P, PACK, M], F32)
        out_rows = out_0.rearrange("(p t) m -> p t m", t=PACK)
        for t in PLACES:
            narrow = bank(f"narrow_{t}", [P, J], t)
            for e, cols in enumerate(HALVES):
                product(narrow[:, cols], t, users_codes[e][:], users_scales[e][:])
            table = tile(f"table_{t}", [P, J], F32)
            run_max = tile(f"run_max_{t}", [P, N], F32)
            nc.vector.tensor_tensor(table[:], narrow[:], wide_listed[t], MAX)
            nc.vector.tensor_reduce(run_max[:], table[:].rearrange("p (n r) -> p n r", r=RUN), AXIS_X, MAX)
            nc.scalar.activation(placed[t][:].indirect(run_list[:]), run_max[:], COPY)
            if t < 2:
                nc.gpsimd.tensor_tensor(result[:, t, :], old_f32[:, t, :], placed[t][:], ADD)
            else:
                for cols in HALVES[::-1] if t == last else (slice(0, M),):
                    nc.vector.tensor_tensor(result[:, t, cols], old_f32[:, t, cols], placed[t][:, cols], ADD)
            nc.sync.dma_start(out_rows[:, t, :], result[:, t, :])

        result_codes = tile("result_codes", [P, M], U32)
        result_scales = tile("result_scales", [P, M], U8)
        out_words = out_1[0].rearrange("p c r -> p (c r)").bitcast(I32)
        for copy, cols in zip(half_copies, HALVES):
            result_bf16 = tile(f"result_bf16_{cols.start}", [P, WIDTH, PACK], BF16)
            interleave(copy, result_bf16[:], result[:, :, cols])
            quantize(nc, result_codes[:, cols], result_scales[:, cols], result_bf16[:])
            nc.sync.dma_start(out_words[:, cols], result_codes[:, cols].bitcast(I32))
        for q in range(4):
            queue = nc.sync if q % 2 else nc.scalar
            queue.dma_start(
                out_2[0, 4 * q : 4 * q + 4, :].bitcast(I32),
                result_scales[32 * q : 32 * q + 4, :].bitcast(I32),
            )
